import numpy as np
import ml_dtypes


def mxq(x, axis, fmt="e4m3"):
    dtype, down = {"e4m3": (ml_dtypes.float8_e4m3fn, 7), "e5m2": (ml_dtypes.float8_e5m2, 14)}[fmt]
    v = np.moveaxis(np.asarray(x, np.float32).astype(ml_dtypes.bfloat16).astype(np.float64), axis, -1)
    blocks = v.reshape(v.shape[:-1] + (-1, 32))
    amax = np.abs(blocks).max(-1, keepdims=True)
    byte = np.maximum(np.where(amax > 0, np.frexp(amax)[1] - 1 + 127, 0) - down, 1)
    scale = np.exp2(byte - 127.0)
    codes = (blocks / scale).astype(np.float32).astype(dtype).astype(np.float64)
    return np.moveaxis((codes * scale).reshape(v.shape), -1, axis)


WIDE = False


def mx_kscale(k):
    if not WIDE:
        return np.ones(k)
    levels = np.array([10, -10, 5, -5, 0])
    if k % 512:
        return np.exp2(np.random.permutation(np.resize(levels, k // 32))).repeat(32)
    a = np.empty((k // 512, 16))
    for p in range(k // 512):
        a[p, :8] = np.random.permutation(np.resize(levels, 8))
        for g in range(8):
            far = levels[np.abs(levels - a[p, g]) >= 10]
            a[p, g + 8] = far[np.random.randint(len(far))]
    return np.exp2(a.ravel()).repeat(32)


def f64(x):
    return np.asarray(x).astype(np.float64)


def striped(idx):
    return np.tile(idx.reshape(-1, 16).T, (8, 1)).astype(np.uint16)


def unstriped(offs):
    return offs[:16].T.reshape(-1).astype(np.int64)


def gelu(v):
    return 0.5 * v * (1.0 + np.tanh(np.sqrt(2.0 / np.pi) * (v + 0.044715 * v**3)))


K, T, E, C, H, N = 1024, 768, 2, 256, 1024, 256


def by_expert(wq, xq):
    return np.concatenate([wq[e].T @ xq[:, e * C:(e + 1) * C] for e in range(E)], axis=1)


def setup_inputs():
    n = np.random.standard_normal
    s = mx_kscale(K)[:, None]
    u = mx_kscale(H)
    return {
        "xT": (n((K, T)) * s).astype(np.float32),
        "w1": (n((E, K, H)) / np.sqrt(K) / s[None]).astype(np.float32),
        "w3": (n((E, K, H)) / np.sqrt(K) / s[None] * u[None, None, :]).astype(np.float32),
        "w2": (n((E, H, N)) / np.sqrt(H) / u[None, :, None]).astype(np.float32),
        "gate": np.tile(np.random.uniform(0.2, 1.0, E * C), (N, 1)).astype(np.float32),
        "offs": striped(np.random.permutation(T)[:E * C]),
    }


def reference(xT, w1, w3, w2, gate, offs):
    idx = unstriped(offs)
    xq = mxq(f64(xT)[:, idx], 0, "e4m3")
    h = gelu(by_expert(mxq(f64(w1), 1, "e4m3"), xq))
    h = h * by_expert(mxq(f64(w3), 1, "e4m3"), xq)
    y = by_expert(mxq(f64(w2), 1, "e4m3"), mxq(h, 0, "e4m3"))
    out = np.zeros((N, T))
    out[:, idx] = f64(gate) * y
    return out

@@ -1,0 +1,262 @@
+from contextlib import ExitStack
+
+import concourse.mybir as mybir
+
+K, T, E, C, H, N = 1024, 768, 2, 256, 1024, 256
+FLOPS = 2 * E * C * (2 * K * H + H * N)
+
+F32 = mybir.dt.float32
+BF16 = mybir.dt.bfloat16
+U32 = mybir.dt.uint32
+U16 = mybir.dt.uint16
+U8 = mybir.dt.uint8
+FP8X4 = mybir.dt.float8_e4m3fn_x4
+GELU = mybir.ActivationFunctionType.Gelu_apprx_tanh
+MULT = mybir.AluOpType.mult
+
+P = 128
+J = 4
+PASS = P * J
+PASSES = K // PASS
+GROUP = 512
+HALF = 128
+
+
+def tile_routed_moe_kernel(tc, xT, w1, w3, w2, gate, offs, out):
+    nc = tc.nc
+    with ExitStack() as ctx:
+        keep = ctx.enter_context(tc.tile_pool(name="keep", bufs=1))
+        raws = ctx.enter_context(tc.tile_pool(name="raws", bufs=6))
+        work = ctx.enter_context(tc.tile_pool(name="work", bufs=4))
+        psum = ctx.enter_context(tc.psum_pool(name="psum", bufs=6))
+        psum_y = ctx.enter_context(tc.psum_pool(name="psum_y", bufs=2))
+
+        offsets = keep.tile([P, E * C // 16], U16, name="offsets")
+        gates = keep.tile([P, N // P, E * C], F32, name="gates")
+        windows = [keep.tile([P, T], F32, name=f"window{b}") for b in range(N // P)]
+        warm = keep.tile([P, 1], F32, name="warm")
+        x_words = [keep.tile([P, T], U32, name=f"x_words{s}", align_bytes=64) for s in range(PASSES)]
+        x_bytes = keep.tile([P, T], U8, name="x_bytes", align_bytes=64)
+        g_words = keep.tile([P, PASSES, E * C], U32, name="g_words", align_bytes=64)
+        g_bytes = keep.tile([P, E * C], U8, name="g_bytes", align_bytes=64)
+
+        def load_x(s):
+            raw = raws.tile([P, J, T], F32, tag="raw", name=f"raw_x{s}")
+            nc.sync.dma_start(out=raw[:], in_=xT[s * PASS : (s + 1) * PASS, :].rearrange("(p j) c -> p j c", j=J))
+            return raw
+
+        def load_w(w, e, s, c0, c1, label):
+            raw = raws.tile([P, J, c1 - c0], F32, tag="raw", name=f"raw_{label}_{e}_{s}_{c0}")
+            nc.sync.dma_start(out=raw[:], in_=w[e, s * PASS : (s + 1) * PASS, c0:c1].rearrange("(p j) c -> p j c", j=J))
+            return raw
+
+        def load_w2(e, s):
+            raw = raws.tile([P, J, N], F32, tag="raw2", bufs=4, name=f"raw_w2_{e}_{s}")
+            nc.sync.dma_start(out=raw[:], in_=w2[e, s * PASS : (s + 1) * PASS, :].rearrange("(p j) c -> p j c", j=J))
+            return raw
+
+        def load_gate(e):
+            nc.sync.dma_start(
+                out=gates[:, :, e * C : (e + 1) * C],
+                in_=gate[:, e * C : (e + 1) * C].rearrange("(b p) c -> p b c", p=P),
+            )
+
+        def copy_split(dst, src, total, cut):
+            if cut > 0:
+                nc.scalar.copy(out=dst[:, 0:cut], in_=src[:, 0:cut])
+            if cut < total:
+                nc.vector.tensor_copy(out=dst[:, cut:total], in_=src[:, cut:total])
+
+        def plain_views(grouped, raw):
+            return (
+                grouped.rearrange("p (c i j) -> p c j i", i=4, j=J),
+                raw.rearrange("p j (c i) -> p c j i", i=4),
+            )
+
+        def permuted_views(grouped, raw):
+            return (
+                grouped.rearrange("p (t m j) -> p m j t", t=4, j=J),
+                raw.rearrange("p j (m t) -> p m j t", t=4),
+            )
+
+        w_words, w_bytes = {}, {}
+
+        X_CUTS = ((0, 512), (512, 768))
+
+        def inter_x(s, raw, cuts):
+            parts = []
+            for (c0, c1), cut in zip(X_CUTS, cuts):
+                grouped = work.tile([P, (c1 - c0) * J], BF16, tag="grouped", bufs=6, name=f"grouped_x{s}_{c0}", align_bytes=64)
+                dst, src = plain_views(grouped[:], raw[:, :, c0:c1])
+                copy_split(dst, src, (c1 - c0) // 4, cut)
+                parts.append(grouped)
+            return parts
+
+        def quant_x(s, parts):
+            for (c0, c1), grouped in zip(X_CUTS, parts):
+                nc.vector.quantize_mx(
+                    out=x_words[s][:, c0:c1].bitcast(FP8X4), scales=x_bytes[4 * s : P, c0:c1], in_=grouped[:]
+                )
+
+        def gather_x(s):
+            nc.vector.tensor_copy(g_words[:, s, :], x_words[s][:].indirect(offsets[:]))
+            if s == PASSES - 1:
+                nc.vector.tensor_copy(g_bytes[:], x_bytes[:].indirect(offsets[:]))
+
+        def new_codes(key, width):
+            label = "_".join(str(k) for k in key)
+            w_words[key] = keep.tile([P, width], U32, name=f"words_{label}", align_bytes=64)
+            w_bytes[key] = keep.tile([P, width], U8, name=f"bytes_{label}", align_bytes=64)
+
+        def inter_w(raw_cols, cut):
+            grouped = work.tile([P, GROUP * J], BF16, tag="grouped", bufs=6, name="grouped", align_bytes=64)
+            dst, src = permuted_views(grouped[:], raw_cols)
+            copy_split(dst, src, GROUP // 4, cut)
+            return grouped
+
+        def quant_w(key, g, grouped):
+            cols = slice(g * GROUP, (g + 1) * GROUP)
+            nc.vector.quantize_mx(out=w_words[key][:, cols].bitcast(FP8X4), scales=w_bytes[key][:, cols], in_=grouped[:])
+
+        def do_w2(e, s, raw, cut):
+            grouped = work.tile([P, N * J], BF16, bufs=2, name="grouped2", align_bytes=64)
+            dst, src = plain_views(grouped[:], raw[:])
+            copy_split(dst, src, N // 4, cut)
+            key = ("w2", e, s)
+            new_codes(key, N)
+            nc.vector.quantize_mx(out=w_words[key][:].bitcast(FP8X4), scales=w_bytes[key][:], in_=grouped[:])
+
+        def mm1(label, e, g, h):
+            acc = psum.tile([P, 4, HALF], F32, name="acc")
+            cols = slice(e * C + h * HALF, e * C + (h + 1) * HALF)
+            for t in range(4):
+                rows = slice(g * GROUP + t * P, g * GROUP + (t + 1) * P)
+                for s in range(PASSES):
+                    key = (label, e, s)
+                    nc.tensor.matmul_mx(
+                        out=acc[:, t, :],
+                        lhsT=w_words[key][:, rows].bitcast(FP8X4),
+                        lhsT_scale=w_bytes[key][:, rows],
+                        rhs=g_words[:, s, cols].bitcast(FP8X4),
+                        rhs_scale=g_bytes[4 * s : P, cols],
+                        start=(s == 0),
+                        stop=(s == PASSES - 1),
+                    )
+            return acc
+
+        gelus, hiddens, h_words, h_bytes = {}, {}, {}, {}
+
+        def first_half(e, g):
+            for h in range(2):
+                acc = mm1("w1", e, g, h)
+                act = work.tile([P, HALF, 4], F32, name="act")
+                nc.scalar.activation(act[:], acc[:].rearrange("p t n -> p n t"), GELU)
+                gelus[(e, g, h)] = act
+
+        def second_half(e, g):
+            hid = work.tile([P, C, 4], BF16, bufs=2, name="hid", align_bytes=64)
+            for h in range(2):
+                acc = mm1("w3", e, g, h)
+                nc.vector.tensor_tensor(
+                    hid[:, h * HALF : (h + 1) * HALF, :], acc[:].rearrange("p t n -> p n t"), gelus[(e, g, h)][:], MULT
+                )
+            hiddens[(e, g)] = hid
+
+        def quant_h(e, g):
+            h_words[(e, g)] = keep.tile([P, C], U32, name=f"h_words_{e}_{g}", align_bytes=64)
+            h_bytes[(e, g)] = keep.tile([P, C], U8, name=f"h_bytes_{e}_{g}", align_bytes=64)
+            nc.vector.quantize_mx(
+                out=h_words[(e, g)][:].bitcast(FP8X4),
+                scales=h_bytes[(e, g)][:],
+                in_=hiddens[(e, g)][:].rearrange("p n t -> p (n t)"),
+            )
+
+        def finish(e):
+            ys = []
+            for b in range(N // P):
+                y = psum_y.tile([P, C], F32, name="y")
+                rows = slice(b * P, (b + 1) * P)
+                for g in range(H // GROUP):
+                    nc.tensor.matmul_mx(
+                        out=y[:],
+                        lhsT=w_words[("w2", e, g)][:, rows].bitcast(FP8X4),
+                        lhsT_scale=w_bytes[("w2", e, g)][:, rows],
+                        rhs=h_words[(e, g)][:].bitcast(FP8X4),
+                        rhs_scale=h_bytes[(e, g)][:],
+                        start=(g == 0),
+                        stop=(g == H // GROUP - 1),
+                    )
+                ys.append(y)
+            weighted = []
+            for b in range(N // P):
+                part = work.tile([P, C], F32, name="weighted")
+                nc.vector.tensor_tensor(part[:], ys[b][:], gates[:, b, e * C : (e + 1) * C], MULT)
+                weighted.append(part)
+            for b in range(N // P):
+                nc.vector.tensor_copy(windows[b][:].indirect(offsets[:, e * C // 16 : (e + 1) * C // 16]), weighted[b][:])
+                if e == E - 1:
+                    nc.sync.dma_start(out=out[b * P : (b + 1) * P, :], in_=windows[b][:])
+
+        nc.sync.dma_start(offsets[:], offs)
+        raw_x = [load_x(s) for s in range(PASSES)]
+        raw_w, raw_w2 = {}, {}
+
+        def load_chunk(chunk):
+            label, e, s = chunk
+            w = w1 if label == "w1" else w3
+            if label == "w2":
+                raw_w2[(e, s)] = load_w2(e, s)
+                if s == PASSES - 1:
+                    load_gate(e)
+            elif chunk == ("w3", E - 1, PASSES - 1):
+                for g in range(2):
+                    raw_w[chunk + (g,)] = load_w(w, e, s, g * GROUP, (g + 1) * GROUP, label)
+            else:
+                raw = load_w(w, e, s, 0, H, label)
+                for g in range(2):
+                    raw_w[chunk + (g,)] = raw
+
+        chunks = [(label, e, s) for e in range(E) for label in ("w1", "w3", "w2") for s in range(PASSES)]
+        for chunk in chunks[0:4]:
+            load_chunk(chunk)
+
+        nc.vector.memset(warm[:], 0.0)
+        hot = keep.tile([P, 1], F32, name="hot")
+        nc.scalar.activation(hot[:], warm[:], GELU)
+        for b in range(N // P):
+            nc.vector.memset(windows[b][:], 0.0)
+
+        gx0 = inter_x(0, raw_x[0], (76, 38))
+        gx1 = inter_x(1, raw_x[1], (76, 38))
+        quant_x(0, gx0)
+        gather_x(0)
+        quant_x(1, gx1)
+        pending = [lambda: gather_x(1)]
+        for k, chunk in enumerate(chunks):
+            if k + 4 < len(chunks):
+                load_chunk(chunks[k + 4])
+            label, e, s = chunk
+            if label == "w2":
+                do_w2(e, s, raw_w2[(e, s)], 64)
+                parts = []
+            else:
+                new_codes(chunk, H)
+                parts = []
+                for g in range(2):
+                    raw = raw_w[chunk + (g,)]
+                    cols = raw[:] if chunk == ("w3", E - 1, PASSES - 1) else raw[:, :, g * GROUP : (g + 1) * GROUP]
+                    parts.append(inter_w(cols, 72 if label == "w1" or e < E - 1 else (56, 32)[s]))
+            for todo in pending:
+                todo()
+            pending = []
+            for g, part in enumerate(parts):
+                quant_w(chunk, g, part)
+            if s == PASSES - 1:
+                if label == "w1":
+                    pending = [lambda e=e, g=g: first_half(e, g) for g in range(2)]
+                elif label == "w3":
+                    pending = [lambda e=e, g=g: second_half(e, g) for g in range(2)] + [lambda e=e, g=g: quant_h(e, g) for g in range(2)]
+                else:
+                    pending = [lambda e=e: finish(e)]
+        for todo in pending:
+            todo()

@@ -20,13 +20,35 @@ PASS = P * J
 PASSES = K // PASS
 GROUP = 512
 HALF = 128
+SHARE = {
+    ("w1", 0, 0, 0): 128,
+    ("w1", 0, 0, 1): 128,
+    ("w1", 0, 1, 0): 56,
+    ("w1", 0, 1, 1): 80,
+    ("w1", 1, 0, 0): 128,
+    ("w1", 1, 0, 1): 128,
+    ("w1", 1, 1, 0): 56,
+    ("w1", 1, 1, 1): 80,
+    ("w3", 0, 0, 0): 0,
+    ("w3", 0, 0, 1): 8,
+    ("w3", 0, 1, 0): 56,
+    ("w3", 0, 1, 1): 56,
+    ("w3", 1, 0, 0): 0,
+    ("w3", 1, 0, 1): 8,
+    ("w3", 1, 1, 0): 96,
+    ("w3", 1, 1, 1): 80,
+}
+SHARE_W2 = (64, 64)
+SHARE_X = ((80, 40), (104, 52))
+D_F, D_M, D_Q, D_Y, D_S = 3, 1, 0, 2, 0
+BUFS = {"raw": 5, "half": 2, "raw2": 4}
 
 
 def tile_routed_moe_kernel(tc, xT, w1, w3, w2, gate, offs, out):
     nc = tc.nc
     with ExitStack() as ctx:
         keep = ctx.enter_context(tc.tile_pool(name="keep", bufs=1))
-        raws = ctx.enter_context(tc.tile_pool(name="raws", bufs=6))
+        raws = ctx.enter_context(tc.tile_pool(name="raws", bufs=1))
         work = ctx.enter_context(tc.tile_pool(name="work", bufs=4))
         psum = ctx.enter_context(tc.psum_pool(name="psum", bufs=6))
         psum_y = ctx.enter_context(tc.psum_pool(name="psum_y", bufs=2))
@@ -41,17 +63,18 @@ def tile_routed_moe_kernel(tc, xT, w1, w3, w2, gate, offs, out):
         g_bytes = keep.tile([P, E * C], U8, name="g_bytes", align_bytes=64)
 
         def load_x(s):
-            raw = raws.tile([P, J, T], F32, tag="raw", name=f"raw_x{s}")
+            raw = raws.tile([P, J, T], F32, tag="raw", bufs=BUFS["raw"], name=f"raw_x{s}")
             nc.sync.dma_start(out=raw[:], in_=xT[s * PASS : (s + 1) * PASS, :].rearrange("(p j) c -> p j c", j=J))
             return raw
 
         def load_w(w, e, s, c0, c1, label):
-            raw = raws.tile([P, J, c1 - c0], F32, tag="raw", name=f"raw_{label}_{e}_{s}_{c0}")
+            tag = "raw" if c1 - c0 == H else "half"
+            raw = raws.tile([P, J, c1 - c0], F32, tag=tag, bufs=BUFS[tag], name=f"raw_{label}_{e}_{s}_{c0}")
             nc.sync.dma_start(out=raw[:], in_=w[e, s * PASS : (s + 1) * PASS, c0:c1].rearrange("(p j) c -> p j c", j=J))
             return raw
 
         def load_w2(e, s):
-            raw = raws.tile([P, J, N], F32, tag="raw2", bufs=4, name=f"raw_w2_{e}_{s}")
+            raw = raws.tile([P, J, N], F32, tag="raw2", bufs=BUFS["raw2"], name=f"raw_w2_{e}_{s}")
             nc.sync.dma_start(out=raw[:], in_=w2[e, s * PASS : (s + 1) * PASS, :].rearrange("(p j) c -> p j c", j=J))
             return raw
 
@@ -118,10 +141,13 @@ def tile_routed_moe_kernel(tc, xT, w1, w3, w2, gate, offs, out):
             cols = slice(g * GROUP, (g + 1) * GROUP)
             nc.vector.quantize_mx(out=w_words[key][:, cols].bitcast(FP8X4), scales=w_bytes[key][:, cols], in_=grouped[:])
 
-        def do_w2(e, s, raw, cut):
+        def inter_w2(raw, cut):
             grouped = work.tile([P, N * J], BF16, bufs=2, name="grouped2", align_bytes=64)
             dst, src = plain_views(grouped[:], raw[:])
             copy_split(dst, src, N // 4, cut)
+            return grouped
+
+        def quant_w2(e, s, grouped):
             key = ("w2", e, s)
             new_codes(key, N)
             nc.vector.quantize_mx(out=w_words[key][:].bitcast(FP8X4), scales=w_bytes[key][:], in_=grouped[:])
@@ -146,21 +172,19 @@ def tile_routed_moe_kernel(tc, xT, w1, w3, w2, gate, offs, out):
 
         gelus, hiddens, h_words, h_bytes = {}, {}, {}, {}
 
-        def first_half(e, g):
-            for h in range(2):
-                acc = mm1("w1", e, g, h)
-                act = work.tile([P, HALF, 4], F32, name="act")
-                nc.scalar.activation(act[:], acc[:].rearrange("p t n -> p n t"), GELU)
-                gelus[(e, g, h)] = act
+        def first_half(e, g, h):
+            acc = mm1("w1", e, g, h)
+            act = work.tile([P, HALF, 4], F32, name="act")
+            nc.scalar.activation(act[:], acc[:].rearrange("p t n -> p n t"), GELU)
+            gelus[(e, g, h)] = act
 
-        def second_half(e, g):
-            hid = work.tile([P, C, 4], BF16, bufs=2, name="hid", align_bytes=64)
-            for h in range(2):
-                acc = mm1("w3", e, g, h)
-                nc.vector.tensor_tensor(
-                    hid[:, h * HALF : (h + 1) * HALF, :], acc[:].rearrange("p t n -> p n t"), gelus[(e, g, h)][:], MULT
-                )
-            hiddens[(e, g)] = hid
+        def second_half(e, g, h):
+            if h == 0:
+                hiddens[(e, g)] = work.tile([P, C, 4], BF16, bufs=2, name="hid", align_bytes=64)
+            acc = mm1("w3", e, g, h)
+            nc.vector.tensor_tensor(
+                hiddens[(e, g)][:, h * HALF : (h + 1) * HALF, :], acc[:].rearrange("p t n -> p n t"), gelus[(e, g, h)][:], MULT
+            )
 
         def quant_h(e, g):
             h_words[(e, g)] = keep.tile([P, C], U32, name=f"h_words_{e}_{g}", align_bytes=64)
@@ -171,92 +195,143 @@ def tile_routed_moe_kernel(tc, xT, w1, w3, w2, gate, offs, out):
                 in_=hiddens[(e, g)][:].rearrange("p n t -> p (n t)"),
             )
 
-        def finish(e):
-            ys = []
-            for b in range(N // P):
-                y = psum_y.tile([P, C], F32, name="y")
-                rows = slice(b * P, (b + 1) * P)
-                for g in range(H // GROUP):
-                    nc.tensor.matmul_mx(
-                        out=y[:],
-                        lhsT=w_words[("w2", e, g)][:, rows].bitcast(FP8X4),
-                        lhsT_scale=w_bytes[("w2", e, g)][:, rows],
-                        rhs=h_words[(e, g)][:].bitcast(FP8X4),
-                        rhs_scale=h_bytes[(e, g)][:],
-                        start=(g == 0),
-                        stop=(g == H // GROUP - 1),
-                    )
-                ys.append(y)
-            weighted = []
-            for b in range(N // P):
-                part = work.tile([P, C], F32, name="weighted")
-                nc.vector.tensor_tensor(part[:], ys[b][:], gates[:, b, e * C : (e + 1) * C], MULT)
-                weighted.append(part)
-            for b in range(N // P):
-                nc.vector.tensor_copy(windows[b][:].indirect(offsets[:, e * C // 16 : (e + 1) * C // 16]), weighted[b][:])
-                if e == E - 1:
-                    nc.sync.dma_start(out=out[b * P : (b + 1) * P, :], in_=windows[b][:])
+        weighted = {}
 
-        nc.sync.dma_start(offsets[:], offs)
-        raw_x = [load_x(s) for s in range(PASSES)]
-        raw_w, raw_w2 = {}, {}
+        def second_layer(e, b):
+            y = psum_y.tile([P, C], F32, name="y")
+            rows = slice(b * P, (b + 1) * P)
+            for g in range(H // GROUP):
+                nc.tensor.matmul_mx(
+                    out=y[:],
+                    lhsT=w_words[("w2", e, g)][:, rows].bitcast(FP8X4),
+                    lhsT_scale=w_bytes[("w2", e, g)][:, rows],
+                    rhs=h_words[(e, g)][:].bitcast(FP8X4),
+                    rhs_scale=h_bytes[(e, g)][:],
+                    start=(g == 0),
+                    stop=(g == H // GROUP - 1),
+                )
+            part = work.tile([P, C], F32, name="weighted")
+            nc.vector.tensor_tensor(part[:], y[:], gates[:, b, e * C : (e + 1) * C], MULT)
+            weighted[(e, b)] = part
 
-        def load_chunk(chunk):
-            label, e, s = chunk
-            w = w1 if label == "w1" else w3
-            if label == "w2":
-                raw_w2[(e, s)] = load_w2(e, s)
-                if s == PASSES - 1:
-                    load_gate(e)
-            elif chunk == ("w3", E - 1, PASSES - 1):
-                for g in range(2):
-                    raw_w[chunk + (g,)] = load_w(w, e, s, g * GROUP, (g + 1) * GROUP, label)
-            else:
-                raw = load_w(w, e, s, 0, H, label)
-                for g in range(2):
-                    raw_w[chunk + (g,)] = raw
+        def scatter(e, b):
+            nc.vector.tensor_copy(windows[b][:].indirect(offsets[:, e * C // 16 : (e + 1) * C // 16]), weighted[(e, b)][:])
+            if e == E - 1:
+                nc.sync.dma_start(out=out[b * P : (b + 1) * P, :], in_=windows[b][:])
 
-        chunks = [(label, e, s) for e in range(E) for label in ("w1", "w3", "w2") for s in range(PASSES)]
-        for chunk in chunks[0:4]:
-            load_chunk(chunk)
+        loads, units = [("x", s) for s in range(PASSES)], []
+        for e in range(E):
+            for label in ("w1", "w3"):
+                for s in range(PASSES):
+                    if (label, e, s) == ("w3", E - 1, PASSES - 1):
+                        loads += [(label, e, s, 0), (label, e, s, 1)]
+                    else:
+                        loads.append((label, e, s))
+                    units += [(label, e, s, 0), (label, e, s, 1)]
+            loads += [("w2", e, s) for s in range(PASSES)] + [("gate", e)]
+            units += [("w2", e, s) for s in range(PASSES)]
+        raw_of, in_use = {}, {"raw": 0, "half": 0, "raw2": 0, None: 0}
+        weights = {"w1": w1, "w3": w3}
 
+        def tag_of(load):
+            if load[0] == "gate":
+                return None
+            if load[0] == "w2":
+                return "raw2"
+            return "half" if len(load) == 4 else "raw"
+
+        def pump():
+            while loads:
+                load = loads[0]
+                tag = tag_of(load)
+                if tag is not None and in_use[tag] == BUFS[tag]:
+                    return
+                in_use[tag] += 1
+                loads.remove(load)
+                if load[0] == "x":
+                    raw_of[load] = load_x(load[1])
+                    if load[1] == PASSES - 1:
+                        nc.sync.dma_start(offsets[:], offs)
+                elif load[0] == "gate":
+                    load_gate(load[1])
+                elif load[0] == "w2":
+                    raw_of[load] = load_w2(load[1], load[2])
+                elif len(load) == 4:
+                    g = load[3]
+                    raw_of[load] = load_w(weights[load[0]], load[1], load[2], g * GROUP, (g + 1) * GROUP, load[0])
+                else:
+                    raw_of[load] = load_w(weights[load[0]], load[1], load[2], 0, H, load[0])
+
+        pump()
         nc.vector.memset(warm[:], 0.0)
         hot = keep.tile([P, 1], F32, name="hot")
         nc.scalar.activation(hot[:], warm[:], GELU)
         for b in range(N // P):
             nc.vector.memset(windows[b][:], 0.0)
 
-        gx0 = inter_x(0, raw_x[0], (76, 38))
-        gx1 = inter_x(1, raw_x[1], (76, 38))
+        def interleave_unit(unit):
+            if unit[0] == "w2":
+                in_use["raw2"] -= 1
+                return inter_w2(raw_of[unit], SHARE_W2[unit[1]])
+            label, e, s, g = unit
+            cut = SHARE[unit]
+            if unit in raw_of:
+                in_use["half"] -= 1
+                return inter_w(raw_of[unit][:], cut)
+            if g == 1:
+                in_use["raw"] -= 1
+            return inter_w(raw_of[unit[0:3]][:, :, g * GROUP : (g + 1) * GROUP], cut)
+
+        def quantise_unit(unit, grouped):
+            if unit[0] == "w2":
+                quant_w2(unit[1], unit[2], grouped)
+            else:
+                key = unit[0:3]
+                if key not in w_words:
+                    new_codes(key, H)
+                quant_w(key, unit[3], grouped)
+
+        gx0 = inter_x(0, raw_of[("x", 0)], SHARE_X[0])
+        in_use["raw"] -= 1
         quant_x(0, gx0)
+        gx1 = inter_x(1, raw_of[("x", 1)], SHARE_X[1])
+        in_use["raw"] -= 1
+        pump()
         gather_x(0)
         quant_x(1, gx1)
-        pending = [lambda: gather_x(1)]
-        for k, chunk in enumerate(chunks):
-            if k + 4 < len(chunks):
-                load_chunk(chunks[k + 4])
-            label, e, s = chunk
-            if label == "w2":
-                do_w2(e, s, raw_w2[(e, s)], 64)
-                parts = []
-            else:
-                new_codes(chunk, H)
-                parts = []
-                for g in range(2):
-                    raw = raw_w[chunk + (g,)]
-                    cols = raw[:] if chunk == ("w3", E - 1, PASSES - 1) else raw[:, :, g * GROUP : (g + 1) * GROUP]
-                    parts.append(inter_w(cols, 72 if label == "w1" or e < E - 1 else (56, 32)[s]))
-            for todo in pending:
+        gather_x(1)
+
+        due = {}
+
+        def later(k, todo):
+            due.setdefault(k, []).append(todo)
+
+        hidden_at = {}
+        for k in range(len(units) + 6):
+            unit = units[k] if k < len(units) else None
+            if unit is not None:
+                grouped = interleave_unit(unit)
+                pump()
+            for todo in due.get(k, []):
                 todo()
-            pending = []
-            for g, part in enumerate(parts):
-                quant_w(chunk, g, part)
-            if s == PASSES - 1:
-                if label == "w1":
-                    pending = [lambda e=e, g=g: first_half(e, g) for g in range(2)]
-                elif label == "w3":
-                    pending = [lambda e=e, g=g: second_half(e, g) for g in range(2)] + [lambda e=e, g=g: quant_h(e, g) for g in range(2)]
-                else:
-                    pending = [lambda e=e: finish(e)]
-        for todo in pending:
-            todo()
+            if unit is None:
+                continue
+            quantise_unit(unit, grouped)
+            if unit[0] == "w2":
+                if unit[2] == 1:
+                    e = unit[1]
+                    wait = max(k, hidden_at[e]) + D_Y if e == 0 else max(k + 1, hidden_at[e])
+                    for b in range(2):
+                        later(wait, lambda e=e, b=b: second_layer(e, b))
+                    for b in range(2):
+                        later(wait + (D_S if e == 0 else 0), lambda e=e, b=b: scatter(e, b))
+            elif unit[2] == 1:
+                e, g = unit[1], unit[3]
+                for h in range(2):
+                    if unit[0] == "w1":
+                        later(k + D_F, lambda e=e, g=g, h=h: first_half(e, g, h))
+                    else:
+                        later(k + D_M, lambda e=e, g=g, h=h: second_half(e, g, h))
+                if unit[0] == "w3":
+                    later(k + D_M + D_Q, lambda e=e, g=g: quant_h(e, g))
+                    hidden_at[e] = k + D_M + D_Q

from contextlib import ExitStack

import concourse.mybir as mybir

K, T, E, C, H, N = 1024, 768, 2, 256, 1024, 256
FLOPS = 2 * E * C * (2 * K * H + H * N)

F32 = mybir.dt.float32
BF16 = mybir.dt.bfloat16
U32 = mybir.dt.uint32
U16 = mybir.dt.uint16
U8 = mybir.dt.uint8
FP8X4 = mybir.dt.float8_e4m3fn_x4
GELU = mybir.ActivationFunctionType.Gelu_apprx_tanh
MULT = mybir.AluOpType.mult

P = 128
J = 4
PASS = P * J
PASSES = K // PASS
GROUP = 512
HALF = 128
SHARE = {
    ("w1", 0, 0, 0): 128,
    ("w1", 0, 0, 1): 128,
    ("w1", 0, 1, 0): 56,
    ("w1", 0, 1, 1): 80,
    ("w1", 1, 0, 0): 128,
    ("w1", 1, 0, 1): 128,
    ("w1", 1, 1, 0): 56,
    ("w1", 1, 1, 1): 80,
    ("w3", 0, 0, 0): 0,
    ("w3", 0, 0, 1): 8,
    ("w3", 0, 1, 0): 56,
    ("w3", 0, 1, 1): 56,
    ("w3", 1, 0, 0): 0,
    ("w3", 1, 0, 1): 8,
    ("w3", 1, 1, 0): 96,
    ("w3", 1, 1, 1): 80,
}
SHARE_W2 = (64, 64)
SHARE_X = ((80, 40), (104, 52))
D_F, D_M, D_Q, D_Y, D_S = 3, 1, 0, 2, 0
BUFS = {"raw": 5, "half": 2, "raw2": 4}


def tile_routed_moe_kernel(tc, xT, w1, w3, w2, gate, offs, out):
    nc = tc.nc
    with ExitStack() as ctx:
        keep = ctx.enter_context(tc.tile_pool(name="keep", bufs=1))
        raws = ctx.enter_context(tc.tile_pool(name="raws", bufs=1))
        work = ctx.enter_context(tc.tile_pool(name="work", bufs=4))
        psum = ctx.enter_context(tc.psum_pool(name="psum", bufs=6))
        psum_y = ctx.enter_context(tc.psum_pool(name="psum_y", bufs=2))

        offsets = keep.tile([P, E * C // 16], U16, name="offsets")
        gates = keep.tile([P, N // P, E * C], F32, name="gates")
        windows = [keep.tile([P, T], F32, name=f"window{b}") for b in range(N // P)]
        warm = keep.tile([P, 1], F32, name="warm")
        x_words = [keep.tile([P, T], U32, name=f"x_words{s}", align_bytes=64) for s in range(PASSES)]
        x_bytes = keep.tile([P, T], U8, name="x_bytes", align_bytes=64)
        g_words = keep.tile([P, PASSES, E * C], U32, name="g_words", align_bytes=64)
        g_bytes = keep.tile([P, E * C], U8, name="g_bytes", align_bytes=64)

        def load_x(s):
            raw = raws.tile([P, J, T], F32, tag="raw", bufs=BUFS["raw"], name=f"raw_x{s}")
            nc.sync.dma_start(out=raw[:], in_=xT[s * PASS : (s + 1) * PASS, :].rearrange("(p j) c -> p j c", j=J))
            return raw

        def load_w(w, e, s, c0, c1, label):
            tag = "raw" if c1 - c0 == H else "half"
            raw = raws.tile([P, J, c1 - c0], F32, tag=tag, bufs=BUFS[tag], name=f"raw_{label}_{e}_{s}_{c0}")
            nc.sync.dma_start(out=raw[:], in_=w[e, s * PASS : (s + 1) * PASS, c0:c1].rearrange("(p j) c -> p j c", j=J))
            return raw

        def load_w2(e, s):
            raw = raws.tile([P, J, N], F32, tag="raw2", bufs=BUFS["raw2"], name=f"raw_w2_{e}_{s}")
            nc.sync.dma_start(out=raw[:], in_=w2[e, s * PASS : (s + 1) * PASS, :].rearrange("(p j) c -> p j c", j=J))
            return raw

        def load_gate(e):
            nc.sync.dma_start(
                out=gates[:, :, e * C : (e + 1) * C],
                in_=gate[:, e * C : (e + 1) * C].rearrange("(b p) c -> p b c", p=P),
            )

        def copy_split(dst, src, total, cut):
            if cut > 0:
                nc.scalar.copy(out=dst[:, 0:cut], in_=src[:, 0:cut])
            if cut < total:
                nc.vector.tensor_copy(out=dst[:, cut:total], in_=src[:, cut:total])

        def plain_views(grouped, raw):
            return (
                grouped.rearrange("p (c i j) -> p c j i", i=4, j=J),
                raw.rearrange("p j (c i) -> p c j i", i=4),
            )

        def permuted_views(grouped, raw):
            return (
                grouped.rearrange("p (t m j) -> p m j t", t=4, j=J),
                raw.rearrange("p j (m t) -> p m j t", t=4),
            )

        w_words, w_bytes = {}, {}

        X_CUTS = ((0, 512), (512, 768))

        def inter_x(s, raw, cuts):
            parts = []
            for (c0, c1), cut in zip(X_CUTS, cuts):
                grouped = work.tile([P, (c1 - c0) * J], BF16, tag="grouped", bufs=6, name=f"grouped_x{s}_{c0}", align_bytes=64)
                dst, src = plain_views(grouped[:], raw[:, :, c0:c1])
                copy_split(dst, src, (c1 - c0) // 4, cut)
                parts.append(grouped)
            return parts

        def quant_x(s, parts):
            for (c0, c1), grouped in zip(X_CUTS, parts):
                nc.vector.quantize_mx(
                    out=x_words[s][:, c0:c1].bitcast(FP8X4), scales=x_bytes[4 * s : P, c0:c1], in_=grouped[:]
                )

        def gather_x(s):
            nc.vector.tensor_copy(g_words[:, s, :], x_words[s][:].indirect(offsets[:]))
            if s == PASSES - 1:
                nc.vector.tensor_copy(g_bytes[:], x_bytes[:].indirect(offsets[:]))

        def new_codes(key, width):
            label = "_".join(str(k) for k in key)
            w_words[key] = keep.tile([P, width], U32, name=f"words_{label}", align_bytes=64)
            w_bytes[key] = keep.tile([P, width], U8, name=f"bytes_{label}", align_bytes=64)

        def inter_w(raw_cols, cut):
            grouped = work.tile([P, GROUP * J], BF16, tag="grouped", bufs=6, name="grouped", align_bytes=64)
            dst, src = permuted_views(grouped[:], raw_cols)
            copy_split(dst, src, GROUP // 4, cut)
            return grouped

        def quant_w(key, g, grouped):
            cols = slice(g * GROUP, (g + 1) * GROUP)
            nc.vector.quantize_mx(out=w_words[key][:, cols].bitcast(FP8X4), scales=w_bytes[key][:, cols], in_=grouped[:])

        def inter_w2(raw, cut):
            grouped = work.tile([P, N * J], BF16, bufs=2, name="grouped2", align_bytes=64)
            dst, src = plain_views(grouped[:], raw[:])
            copy_split(dst, src, N // 4, cut)
            return grouped

        def quant_w2(e, s, grouped):
            key = ("w2", e, s)
            new_codes(key, N)
            nc.vector.quantize_mx(out=w_words[key][:].bitcast(FP8X4), scales=w_bytes[key][:], in_=grouped[:])

        def mm1(label, e, g, h):
            acc = psum.tile([P, 4, HALF], F32, name="acc")
            cols = slice(e * C + h * HALF, e * C + (h + 1) * HALF)
            for t in range(4):
                rows = slice(g * GROUP + t * P, g * GROUP + (t + 1) * P)
                for s in range(PASSES):
                    key = (label, e, s)
                    nc.tensor.matmul_mx(
                        out=acc[:, t, :],
                        lhsT=w_words[key][:, rows].bitcast(FP8X4),
                        lhsT_scale=w_bytes[key][:, rows],
                        rhs=g_words[:, s, cols].bitcast(FP8X4),
                        rhs_scale=g_bytes[4 * s : P, cols],
                        start=(s == 0),
                        stop=(s == PASSES - 1),
                    )
            return acc

        gelus, hiddens, h_words, h_bytes = {}, {}, {}, {}

        def first_half(e, g, h):
            acc = mm1("w1", e, g, h)
            act = work.tile([P, HALF, 4], F32, name="act")
            nc.scalar.activation(act[:], acc[:].rearrange("p t n -> p n t"), GELU)
            gelus[(e, g, h)] = act

        def second_half(e, g, h):
            if h == 0:
                hiddens[(e, g)] = work.tile([P, C, 4], BF16, bufs=2, name="hid", align_bytes=64)
            acc = mm1("w3", e, g, h)
            nc.vector.tensor_tensor(
                hiddens[(e, g)][:, h * HALF : (h + 1) * HALF, :], acc[:].rearrange("p t n -> p n t"), gelus[(e, g, h)][:], MULT
            )

        def quant_h(e, g):
            h_words[(e, g)] = keep.tile([P, C], U32, name=f"h_words_{e}_{g}", align_bytes=64)
            h_bytes[(e, g)] = keep.tile([P, C], U8, name=f"h_bytes_{e}_{g}", align_bytes=64)
            nc.vector.quantize_mx(
                out=h_words[(e, g)][:].bitcast(FP8X4),
                scales=h_bytes[(e, g)][:],
                in_=hiddens[(e, g)][:].rearrange("p n t -> p (n t)"),
            )

        weighted = {}

        def second_layer(e, b):
            y = psum_y.tile([P, C], F32, name="y")
            rows = slice(b * P, (b + 1) * P)
            for g in range(H // GROUP):
                nc.tensor.matmul_mx(
                    out=y[:],
                    lhsT=w_words[("w2", e, g)][:, rows].bitcast(FP8X4),
                    lhsT_scale=w_bytes[("w2", e, g)][:, rows],
                    rhs=h_words[(e, g)][:].bitcast(FP8X4),
                    rhs_scale=h_bytes[(e, g)][:],
                    start=(g == 0),
                    stop=(g == H // GROUP - 1),
                )
            part = work.tile([P, C], F32, name="weighted")
            nc.vector.tensor_tensor(part[:], y[:], gates[:, b, e * C : (e + 1) * C], MULT)
            weighted[(e, b)] = part

        def scatter(e, b):
            nc.vector.tensor_copy(windows[b][:].indirect(offsets[:, e * C // 16 : (e + 1) * C // 16]), weighted[(e, b)][:])
            if e == E - 1:
                nc.sync.dma_start(out=out[b * P : (b + 1) * P, :], in_=windows[b][:])

        loads, units = [("x", s) for s in range(PASSES)], []
        for e in range(E):
            for label in ("w1", "w3"):
                for s in range(PASSES):
                    if (label, e, s) == ("w3", E - 1, PASSES - 1):
                        loads += [(label, e, s, 0), (label, e, s, 1)]
                    else:
                        loads.append((label, e, s))
                    units += [(label, e, s, 0), (label, e, s, 1)]
            loads += [("w2", e, s) for s in range(PASSES)] + [("gate", e)]
            units += [("w2", e, s) for s in range(PASSES)]
        raw_of, in_use = {}, {"raw": 0, "half": 0, "raw2": 0, None: 0}
        weights = {"w1": w1, "w3": w3}

        def tag_of(load):
            if load[0] == "gate":
                return None
            if load[0] == "w2":
                return "raw2"
            return "half" if len(load) == 4 else "raw"

        def pump():
            while loads:
                load = loads[0]
                tag = tag_of(load)
                if tag is not None and in_use[tag] == BUFS[tag]:
                    return
                in_use[tag] += 1
                loads.remove(load)
                if load[0] == "x":
                    raw_of[load] = load_x(load[1])
                    if load[1] == PASSES - 1:
                        nc.sync.dma_start(offsets[:], offs)
                elif load[0] == "gate":
                    load_gate(load[1])
                elif load[0] == "w2":
                    raw_of[load] = load_w2(load[1], load[2])
                elif len(load) == 4:
                    g = load[3]
                    raw_of[load] = load_w(weights[load[0]], load[1], load[2], g * GROUP, (g + 1) * GROUP, load[0])
                else:
                    raw_of[load] = load_w(weights[load[0]], load[1], load[2], 0, H, load[0])

        pump()
        nc.vector.memset(warm[:], 0.0)
        hot = keep.tile([P, 1], F32, name="hot")
        nc.scalar.activation(hot[:], warm[:], GELU)
        for b in range(N // P):
            nc.vector.memset(windows[b][:], 0.0)

        def interleave_unit(unit):
            if unit[0] == "w2":
                in_use["raw2"] -= 1
                return inter_w2(raw_of[unit], SHARE_W2[unit[1]])
            label, e, s, g = unit
            cut = SHARE[unit]
            if unit in raw_of:
                in_use["half"] -= 1
                return inter_w(raw_of[unit][:], cut)
            if g == 1:
                in_use["raw"] -= 1
            return inter_w(raw_of[unit[0:3]][:, :, g * GROUP : (g + 1) * GROUP], cut)

        def quantise_unit(unit, grouped):
            if unit[0] == "w2":
                quant_w2(unit[1], unit[2], grouped)
            else:
                key = unit[0:3]
                if key not in w_words:
                    new_codes(key, H)
                quant_w(key, unit[3], grouped)

        gx0 = inter_x(0, raw_of[("x", 0)], SHARE_X[0])
        in_use["raw"] -= 1
        quant_x(0, gx0)
        gx1 = inter_x(1, raw_of[("x", 1)], SHARE_X[1])
        in_use["raw"] -= 1
        pump()
        gather_x(0)
        quant_x(1, gx1)
        gather_x(1)

        due = {}

        def later(k, todo):
            due.setdefault(k, []).append(todo)

        hidden_at = {}
        for k in range(len(units) + 6):
            unit = units[k] if k < len(units) else None
            if unit is not None:
                grouped = interleave_unit(unit)
                pump()
            for todo in due.get(k, []):
                todo()
            if unit is None:
                continue
            quantise_unit(unit, grouped)
            if unit[0] == "w2":
                if unit[2] == 1:
                    e = unit[1]
                    wait = max(k, hidden_at[e]) + D_Y if e == 0 else max(k + 1, hidden_at[e])
                    for b in range(2):
                        later(wait, lambda e=e, b=b: second_layer(e, b))
                    for b in range(2):
                        later(wait + (D_S if e == 0 else 0), lambda e=e, b=b: scatter(e, b))
            elif unit[2] == 1:
                e, g = unit[1], unit[3]
                for h in range(2):
                    if unit[0] == "w1":
                        later(k + D_F, lambda e=e, g=g, h=h: first_half(e, g, h))
                    else:
                        later(k + D_M, lambda e=e, g=g, h=h: second_half(e, g, h))
                if unit[0] == "w3":
                    later(k + D_M + D_Q, lambda e=e, g=g: quant_h(e, g))
                    hidden_at[e] = k + D_M + D_Q
